import numpy as np
import ml_dtypes


def mxq(x, axis, fmt="e4m3"):
    dtype, down = {"e4m3": (ml_dtypes.float8_e4m3fn, 7), "e5m2": (ml_dtypes.float8_e5m2, 14)}[fmt]
    v = np.moveaxis(np.asarray(x, np.float32).astype(ml_dtypes.bfloat16).astype(np.float64), axis, -1)
    blocks = v.reshape(v.shape[:-1] + (-1, 32))
    amax = np.abs(blocks).max(-1, keepdims=True)
    byte = np.maximum(np.where(amax > 0, np.frexp(amax)[1] - 1 + 127, 0) - down, 1)
    scale = np.exp2(byte - 127.0)
    codes = (blocks / scale).astype(np.float32).astype(dtype).astype(np.float64)
    return np.moveaxis((codes * scale).reshape(v.shape), -1, axis)


WIDE = False


def mx_kscale(k):
    if not WIDE:
        return np.ones(k)
    levels = np.array([10, -10, 5, -5, 0])
    if k % 512:
        return np.exp2(np.random.permutation(np.resize(levels, k // 32))).repeat(32)
    a = np.empty((k // 512, 16))
    for p in range(k // 512):
        a[p, :8] = np.random.permutation(np.resize(levels, 8))
        for g in range(8):
            far = levels[np.abs(levels - a[p, g]) >= 10]
            a[p, g + 8] = far[np.random.randint(len(far))]
    return np.exp2(a.ravel()).repeat(32)


def f64(x):
    return np.asarray(x).astype(np.float64)


def striped(idx):
    return np.tile(idx.reshape(-1, 16).T, (8, 1)).astype(np.uint16)


def unstriped(offs):
    return offs[:16].T.reshape(-1).astype(np.int64)


def striped8(idx):
    return np.concatenate([x.reshape(-1, 16).T for x in idx]).astype(np.uint16)


def runs(offs, k):
    lists = np.stack([offs[16 * r : 16 * r + 16].T.reshape(-1) for r in range(8)]).astype(np.int64)
    return lists[np.arange(k) % 512 // 64]


def pack_weight(w):
    k, n = w.shape
    w = f64(np.asarray(w, np.float32).astype(ml_dtypes.bfloat16)).reshape(k // 32, 32, n)
    amax = np.abs(w).max(1)
    byte = np.clip(np.where(amax > 0, np.frexp(amax)[1] - 1 + 127 - 7, 1), 1, 254)
    scaled = (w * np.exp2(127.0 - byte)[:, None, :]).reshape(k, n).astype(np.float32)
    words = np.ascontiguousarray(scaled.reshape(k // 512, 128, 4, n).transpose(0, 1, 3, 2)).astype(ml_dtypes.float8_e4m3fn).view(np.uint8)
    return words, np.ascontiguousarray(byte.astype(np.uint8).reshape(k // 512, 16, n))


def unpack_weight(words, scales):
    g, p, n, _ = words.shape
    vals = np.ascontiguousarray(words).view(ml_dtypes.float8_e4m3fn).astype(np.float64) * np.repeat(np.exp2(scales.astype(np.float64) - 127.0), 8, axis=1)[..., None]
    return vals.transpose(0, 1, 3, 2).reshape(g * 512, n)


def sigmoid(v):
    return 1.0 / (1.0 + np.exp(-np.maximum(v, -700.0)))


K, T, S, G, H, C, W = 512, 1024, 256, 2048, 512, 512, 192


def setup_inputs():
    n = np.random.standard_normal
    s = mx_kscale(K)[:, None]
    packed_xT = pack_weight(n((K, T)) * s)
    packed_dT = pack_weight(n((K, G)) / s)
    return {
        "x_words": packed_xT[0],
        "x_scales": packed_xT[1],
        "d_words": packed_dT[0],
        "d_scales": packed_dT[1],
        "sl": np.random.uniform(1.0, 2.0, (H, 1)).astype(np.float32),
        "th": (0.5 * n((H, 1))).astype(np.float32),
        "gs": (np.random.uniform(0.5, 1.5, (K, 1)) / s).astype(np.float32),
        "offs": striped8(np.random.randint(0, T, (8, S))),
        "k1": striped8(np.random.randint(0, G, (8, H))),
        "n1": striped8(np.stack([np.random.permutation(S) for _ in range(8)])),
        "n2": striped8(np.stack([np.random.permutation(S) for _ in range(8)])),
        "cand": striped(np.random.permutation(T)[:C]),
        "n3": striped(np.random.permutation(S)[:W]),
        "n4": striped(np.random.permutation(S)[:W]),
    }


def reference(x_words, x_scales, d_words, d_scales, sl, th, gs, offs, k1, n1, n2, cand, n3, n4):
    x_cand = unpack_weight(x_words, x_scales)[:, unstriped(cand)]
    d_k1 = unpack_weight(d_words, d_scales)[np.arange(K)[:, None], runs(k1, K)]
    xq = unpack_weight(x_words, x_scales)[np.arange(K)[:, None], runs(offs, K)]
    h = 0.0625 * (d_k1.T @ xq)
    st = np.maximum(h, h[np.arange(H)[:, None], runs(n1, H)])
    sg = sigmoid(f64(sl) * (st[np.arange(H)[:, None], runs(n2, H)] - f64(th)))
    z = f64(gs) * (st * sg)
    s = 0.0625 * ((x_cand.T @ mxq(z, 0, "e4m3")))
    old = s[:, unstriped(n3)]
    pa = s[:, unstriped(n4)]
    ra = old - (0.5 * pa)
    out = s.copy()
    out[:, unstriped(n3)] = ra
    return out

@@ -1,0 +1,182 @@
+from contextlib import ExitStack
+
+import concourse.mybir as mybir
+
+K, T, S, G, H, C, W = 512, 1024, 256, 2048, 512, 512, 192
+FLOPS = 2 * K * H * S + 2 * K * C * S
+
+F32 = mybir.dt.float32
+BF16 = mybir.dt.bfloat16
+I32 = mybir.dt.int32
+U32 = mybir.dt.uint32
+U16 = mybir.dt.uint16
+U8 = mybir.dt.uint8
+FP8X4 = mybir.dt.float8_e4m3fn_x4
+ALU = mybir.AluOpType
+ACT = mybir.ActivationFunctionType
+
+P = 128
+PACK = 4
+HALF = S // 2
+PER_COL = 16
+
+
+def tile_picked_hpqcehhkdif_none_p_kernel(tc, x_words, x_scales, d_words, d_scales, sl, th, gs, offs, k1, n1, n2, cand, n3, n4, out):
+    nc = tc.nc
+    with ExitStack() as ctx:
+        lists = ctx.enter_context(tc.tile_pool(name="lists", bufs=1))
+        sb = ctx.enter_context(tc.tile_pool(name="sb", bufs=1))
+        psum = ctx.enter_context(tc.psum_pool(name="psum", bufs=1))
+
+        def load_list(src, name):
+            tile = lists.tile(list(src.shape), U16, name=name)
+            nc.sync.dma_start(tile[:], src)
+            return tile
+
+        d_bytes = sb.tile([P, G], U8, align_bytes=64)
+        x_bytes_runs = sb.tile([P, T], U8, align_bytes=64)
+        placed = sb.tile([P, H + S], U8, align_bytes=64)
+        nc.vector.memset(d_bytes[:].bitcast(I32), 0)
+        nc.vector.memset(x_bytes_runs[:].bitcast(I32), 0)
+        x_bytes_cand = sb.tile([P, T], U8, align_bytes=64)
+        nc.vector.memset(placed[:].bitcast(I32), 0)
+        nc.vector.memset(x_bytes_cand[:].bitcast(I32), 0)
+
+        k1_l = load_list(k1, "k1_l")
+        offs_l = load_list(offs, "offs_l")
+        n1_l = load_list(n1, "n1_l")
+        cand_l = load_list(cand, "cand_l")
+        nc.sync.dma_start(d_bytes[:].bitcast(I32)[0:P:8, :], d_scales[0].bitcast(I32))
+        nc.sync.dma_start(x_bytes_runs[:].bitcast(I32)[0:P:8, :], x_scales[0].bitcast(I32))
+        d_tab = sb.tile([P, G], U32, align_bytes=64)
+        x_tab = sb.tile([P, T], U32, align_bytes=64)
+        nc.sync.dma_start(d_tab[:].bitcast(I32), d_words[0].rearrange("p n t -> p (n t)").bitcast(I32))
+        nc.sync.dma_start(x_tab[:].bitcast(I32), x_words[0].rearrange("p n t -> p (n t)").bitcast(I32))
+        n2_l = load_list(n2, "n2_l")
+        n3_l = load_list(n3, "n3_l")
+        n4_l = load_list(n4, "n4_l")
+
+        slope = sb.tile([P, PACK], F32)
+        thresh = sb.tile([P, PACK], F32)
+        gain = sb.tile([P, PACK], F32)
+        nc.gpsimd.dma_start(slope[:], sl.rearrange("(p t) o -> p (t o)", t=PACK))
+        nc.gpsimd.dma_start(thresh[:], th.rearrange("(p t) o -> p (t o)", t=PACK))
+        nc.gpsimd.dma_start(gain[:], gs.rearrange("(p t) o -> p (t o)", t=PACK))
+        for q in range(4):
+            nc.gpsimd.dma_start(x_bytes_cand[:].bitcast(I32)[32 * q : 32 * q + 4, :], x_scales[0].bitcast(I32)[4 * q : 4 * q + 4, :])
+        slope_th = sb.tile([P, PACK], F32)
+        bias = sb.tile([P, PACK], F32)
+        nc.gpsimd.tensor_tensor(slope_th[:], slope[:], thresh[:], ALU.mult)
+        nc.gpsimd.tensor_scalar(bias[:], slope_th[:], -1.0, 0.0, ALU.mult, ALU.add)
+
+        picked_bytes = sb.tile([P, H + S], U8, align_bytes=64)
+        nc.vector.tensor_copy(picked_bytes[:, 0:H], d_bytes[:].indirect(k1_l[:]))
+        nc.vector.tensor_copy(picked_bytes[:, H : H + S], x_bytes_runs[:].indirect(offs_l[:]))
+        for q in range(4):
+            nc.scalar.dma_start(placed[:].bitcast(I32)[32 * q : 32 * q + 4, :], picked_bytes[:].bitcast(I32)[32 * q : 32 * q + 32 : 8, :])
+
+        d_picked = sb.tile([P, H], U32, align_bytes=64)
+        x_picked = sb.tile([P, S], U32, align_bytes=64)
+        nc.vector.tensor_copy(d_picked[:], d_tab[:].indirect(k1_l[:]))
+        nc.vector.tensor_copy(x_picked[:], x_tab[:].indirect(offs_l[:]))
+
+        first_words = sb.tile([P, P], U32, align_bytes=64)
+        first_bytes = sb.tile([P, P], U8, align_bytes=64)
+        rest_words = sb.tile([P, PACK - 1, P], U32, align_bytes=64)
+        rest_bytes = sb.tile([P, PACK - 1, P], U8, align_bytes=64)
+        nc.vector.tensor_copy(first_words[:], d_picked[:, 0:H:PACK])
+        nc.vector.tensor_copy(first_bytes[:], placed[:, 0:H:PACK])
+        nc.vector.tensor_copy(rest_words[:], d_picked[:].rearrange("p (m t) -> p t m", t=PACK)[:, 1:PACK, :])
+        nc.vector.tensor_copy(rest_bytes[:], placed[:, 0:H].rearrange("p (m t) -> p t m", t=PACK)[:, 1:PACK, :])
+        dealt_words = [first_words[:]] + [rest_words[:, t, :] for t in range(PACK - 1)]
+        dealt_bytes = [first_bytes[:]] + [rest_bytes[:, t, :] for t in range(PACK - 1)]
+
+        h = []
+        for t in range(PACK):
+            acc = psum.tile([P, S], F32, name="h_acc%d" % t)
+            nc.tensor.matmul_mx(out=acc[:], lhsT=dealt_words[t].bitcast(FP8X4), lhsT_scale=dealt_bytes[t],
+                                rhs=x_picked[:].bitcast(FP8X4), rhs_scale=placed[:, H : H + S], start=True, stop=True)
+            h_t = sb.tile([P, S], F32, name="h%d" % t)
+            if t == 0:
+                nc.scalar.activation(h_t[:], acc[:], ACT.Copy, scale=0.0625)
+            else:
+                nc.vector.tensor_scalar(h_t[:], acc[:], 0.0625, None, ALU.mult)
+            h.append(h_t)
+
+        st = []
+        for t in range(PACK):
+            other = sb.tile([P, S], F32, align_bytes=64, name="other%d" % t, tag="other%d" % t)
+            for half in range(2):
+                cols = slice(half * HALF, (half + 1) * HALF)
+                entries = slice(half * HALF // PER_COL, (half + 1) * HALF // PER_COL)
+                nc.scalar.activation(other[:, cols], h[t][:].indirect(n1_l[:, entries]), ACT.Copy)
+            st_t = sb.tile([P, S], F32, name="st%d" % t)
+            nc.vector.tensor_tensor(st_t[:], h[t][:], other[:], ALU.max)
+            st.append(st_t)
+
+        cand_words, cand_bytes = [], []
+
+        def pick_candidates(t):
+            entries = slice(t * P // PER_COL, (t + 1) * P // PER_COL)
+            words = sb.tile([P, P], U32, align_bytes=64, name="cand_words%d" % t, tag="other2" if t == 0 else "woven1")
+            scale = sb.tile([P, P], U8, align_bytes=64, name="cand_bytes%d" % t, tag="other3" if t == 0 else "planes1")
+            nc.vector.tensor_copy(words[:], x_tab[:].indirect(cand_l[:, entries]))
+            nc.vector.tensor_copy(scale[:], x_bytes_cand[:].indirect(cand_l[:, entries]))
+            cand_words.append(words)
+            cand_bytes.append(scale)
+
+        pick_candidates(0)
+
+        z_words = sb.tile([P, S], U32, align_bytes=64)
+        z_bytes = sb.tile([P, S], U8, align_bytes=64)
+        for half in range(2):
+            cols = slice(half * HALF, (half + 1) * HALF)
+            entries = slice(half * HALF // PER_COL, (half + 1) * HALF // PER_COL)
+            planes = sb.tile([P, PACK, HALF], BF16, align_bytes=64, name="planes%d" % half, tag="planes%d" % half)
+            for t in range(PACK):
+                sg = sb.tile([P, HALF], F32, align_bytes=64, name="sg%d_%d" % (half, t), tag="sg%d_%d" % (half, t))
+                nc.scalar.activation(sg[:], st[t][:].indirect(n2_l[:, entries]), ACT.Sigmoid,
+                                     scale=slope[:, t : t + 1], bias=bias[:, t : t + 1])
+                nc.vector.scalar_tensor_tensor(planes[:, t, :], st[t][:, cols], gain[:, t : t + 1], sg[:], ALU.mult, ALU.mult)
+            woven = sb.tile([P, HALF, PACK], BF16, align_bytes=64, name="woven%d" % half, tag="woven%d" % half)
+            nc.vector.tensor_copy(woven[:].rearrange("p (c i) t -> p c t i", i=4), planes[:].rearrange("p t (c i) -> p c t i", i=4))
+            nc.vector.quantize_mx(out=z_words[:, cols].bitcast(FP8X4), scales=z_bytes[:, cols],
+                                  in_=woven[:].rearrange("p j t -> p (j t)"))
+
+        s, moved = [], []
+
+        def product(t):
+            acc = psum.tile([P, S], F32, name="s_acc%d" % t)
+            pieces = [slice(0, HALF), slice(HALF, S)] if t == 0 else [slice(0, S)]
+            s_t = sb.tile([P, S], F32, name="s%d" % t)
+            for cols in pieces:
+                nc.tensor.matmul_mx(out=acc[:, cols], lhsT=cand_words[t][:].bitcast(FP8X4), lhsT_scale=cand_bytes[t][:],
+                                    rhs=z_words[:, cols].bitcast(FP8X4), rhs_scale=z_bytes[:, cols], start=True, stop=True)
+                if t == 0:
+                    nc.scalar.activation(s_t[:, cols], acc[:, cols], ACT.Copy, scale=0.0625)
+                else:
+                    nc.vector.tensor_scalar(s_t[:, cols], acc[:, cols], 0.0625, None, ALU.mult)
+            s.append(s_t)
+
+        def fetch(t):
+            old = sb.tile([P, W], F32, name="old%d" % t)
+            partner = sb.tile([P, W], F32, name="partner%d" % t)
+            nc.scalar.activation(old[:], s[t][:].indirect(n3_l[:]), ACT.Copy)
+            nc.scalar.activation(partner[:], s[t][:].indirect(n4_l[:]), ACT.Copy)
+            new = sb.tile([P, W], F32, align_bytes=64, name="new%d" % t)
+            nc.vector.scalar_tensor_tensor(new[:], partner[:], -0.5, old[:], ALU.mult, ALU.add)
+            moved.append(new)
+
+        def put(t):
+            nc.scalar.activation(s[t][:].indirect(n3_l[:]), moved[t][:], ACT.Copy)
+            nc.sync.dma_start(out[t * P : (t + 1) * P, :], s[t][:])
+
+        product(0)
+        for t in range(PACK):
+            if t + 1 < PACK:
+                pick_candidates(t + 1)
+                product(t + 1)
+            fetch(t)
+            if t > 0:
+                put(t - 1)
+        put(PACK - 1)

@@ -56,6 +56,11 @@ def tile_picked_hpqcehhkdif_none_p_kernel(tc, x_words, x_scales, d_words, d_scal
         n3_l = load_list(n3, "n3_l")
         n4_l = load_list(n4, "n4_l")
 
+        warm_in = sb.tile([P, 1], F32)
+        warm_out = sb.tile([P, 1], F32)
+        nc.gpsimd.memset(warm_in[:], 0.0)
+        nc.scalar.activation(warm_out[:], warm_in[:], ACT.Sigmoid)
+
         slope = sb.tile([P, PACK], F32)
         thresh = sb.tile([P, PACK], F32)
         gain = sb.tile([P, PACK], F32)

@@ -36,21 +36,25 @@ def tile_picked_hpqcehhkdif_none_p_kernel(tc, x_words, x_scales, d_words, d_scal
         d_bytes = sb.tile([P, G], U8, align_bytes=64)
         x_bytes_runs = sb.tile([P, T], U8, align_bytes=64)
         placed = sb.tile([P, H + S], U8, align_bytes=64)
-        nc.vector.memset(d_bytes[:].bitcast(I32), 0)
         nc.vector.memset(x_bytes_runs[:].bitcast(I32), 0)
+        nc.vector.memset(d_bytes[:].bitcast(I32), 0)
         x_bytes_cand = sb.tile([P, T], U8, align_bytes=64)
         nc.vector.memset(placed[:].bitcast(I32), 0)
         nc.vector.memset(x_bytes_cand[:].bitcast(I32), 0)
 
-        k1_l = load_list(k1, "k1_l")
-        offs_l = load_list(offs, "offs_l")
-        n1_l = load_list(n1, "n1_l")
-        cand_l = load_list(cand, "cand_l")
-        nc.sync.dma_start(d_bytes[:].bitcast(I32)[0:P:8, :], d_scales[0].bitcast(I32))
-        nc.sync.dma_start(x_bytes_runs[:].bitcast(I32)[0:P:8, :], x_scales[0].bitcast(I32))
+        h = [sb.tile([P, 2 * S], F32, name="h%d" % t) for t in range(PACK)]
+        for t in range(PACK):
+            nc.vector.memset(h[t][:, S : 2 * S], 0.0)
+
         d_tab = sb.tile([P, G], U32, align_bytes=64)
         x_tab = sb.tile([P, T], U32, align_bytes=64)
+        offs_l = load_list(offs, "offs_l")
+        k1_l = load_list(k1, "k1_l")
+        nc.sync.dma_start(x_bytes_runs[:].bitcast(I32)[0:P:8, :], x_scales[0].bitcast(I32))
+        n1_l = load_list(n1, "n1_l")
+        nc.sync.dma_start(d_bytes[:].bitcast(I32)[0:P:8, :], d_scales[0].bitcast(I32))
         nc.sync.dma_start(d_tab[:].bitcast(I32), d_words[0].rearrange("p n t -> p (n t)").bitcast(I32))
+        cand_l = load_list(cand, "cand_l")
         nc.sync.dma_start(x_tab[:].bitcast(I32), x_words[0].rearrange("p n t -> p (n t)").bitcast(I32))
         n2_l = load_list(n2, "n2_l")
         n3_l = load_list(n3, "n3_l")
@@ -75,78 +79,76 @@ def tile_picked_hpqcehhkdif_none_p_kernel(tc, x_words, x_scales, d_words, d_scal
         nc.gpsimd.tensor_scalar(bias[:], slope_th[:], -1.0, 0.0, ALU.mult, ALU.add)
 
         picked_bytes = sb.tile([P, H + S], U8, align_bytes=64)
-        nc.vector.tensor_copy(picked_bytes[:, 0:H], d_bytes[:].indirect(k1_l[:]))
         nc.vector.tensor_copy(picked_bytes[:, H : H + S], x_bytes_runs[:].indirect(offs_l[:]))
+        nc.vector.tensor_copy(picked_bytes[:, 0:H], d_bytes[:].indirect(k1_l[:]))
         for q in range(4):
-            nc.scalar.dma_start(placed[:].bitcast(I32)[32 * q : 32 * q + 4, :], picked_bytes[:].bitcast(I32)[32 * q : 32 * q + 32 : 8, :])
+            (nc.scalar, nc.sync)[q % 2].dma_start(placed[:].bitcast(I32)[32 * q : 32 * q + 4, :], picked_bytes[:].bitcast(I32)[32 * q : 32 * q + 32 : 8, :])
 
         d_picked = sb.tile([P, H], U32, align_bytes=64)
         x_picked = sb.tile([P, S], U32, align_bytes=64)
         nc.vector.tensor_copy(d_picked[:], d_tab[:].indirect(k1_l[:]))
         nc.vector.tensor_copy(x_picked[:], x_tab[:].indirect(offs_l[:]))
 
-        first_words = sb.tile([P, P], U32, align_bytes=64)
-        first_bytes = sb.tile([P, P], U8, align_bytes=64)
-        rest_words = sb.tile([P, PACK - 1, P], U32, align_bytes=64)
-        rest_bytes = sb.tile([P, PACK - 1, P], U8, align_bytes=64)
-        nc.vector.tensor_copy(first_words[:], d_picked[:, 0:H:PACK])
-        nc.vector.tensor_copy(first_bytes[:], placed[:, 0:H:PACK])
-        nc.vector.tensor_copy(rest_words[:], d_picked[:].rearrange("p (m t) -> p t m", t=PACK)[:, 1:PACK, :])
-        nc.vector.tensor_copy(rest_bytes[:], placed[:, 0:H].rearrange("p (m t) -> p t m", t=PACK)[:, 1:PACK, :])
-        dealt_words = [first_words[:]] + [rest_words[:, t, :] for t in range(PACK - 1)]
-        dealt_bytes = [first_bytes[:]] + [rest_bytes[:, t, :] for t in range(PACK - 1)]
+        dealt_words = sb.tile([P, PACK, P], U32, align_bytes=64)
+        dealt_bytes = sb.tile([P, PACK, P], U8, align_bytes=64)
+        for group in (slice(0, 1), slice(1, 2), slice(2, 4)):
+            nc.vector.tensor_copy(dealt_words[:, group, :], d_picked[:].rearrange("p (m t) -> p t m", t=PACK)[:, group, :])
+            nc.vector.tensor_copy(dealt_bytes[:, group, :], placed[:, 0:H].rearrange("p (m t) -> p t m", t=PACK)[:, group, :])
 
-        h = []
         for t in range(PACK):
             acc = psum.tile([P, S], F32, name="h_acc%d" % t)
-            nc.tensor.matmul_mx(out=acc[:], lhsT=dealt_words[t].bitcast(FP8X4), lhsT_scale=dealt_bytes[t],
+            nc.tensor.matmul_mx(out=acc[:], lhsT=dealt_words[:, t, :].bitcast(FP8X4), lhsT_scale=dealt_bytes[:, t, :],
                                 rhs=x_picked[:].bitcast(FP8X4), rhs_scale=placed[:, H : H + S], start=True, stop=True)
-            h_t = sb.tile([P, S], F32, name="h%d" % t)
             if t == 0:
-                nc.scalar.activation(h_t[:], acc[:], ACT.Copy, scale=0.0625)
+                nc.scalar.activation(h[t][:, 0:S], acc[:], ACT.Copy, scale=0.0625)
             else:
-                nc.vector.tensor_scalar(h_t[:], acc[:], 0.0625, None, ALU.mult)
-            h.append(h_t)
+                nc.vector.tensor_scalar(h[t][:, 0:S], acc[:], 0.0625, None, ALU.mult)
 
         st = []
         for t in range(PACK):
             other = sb.tile([P, S], F32, align_bytes=64, name="other%d" % t, tag="other%d" % t)
-            for half in range(2):
-                cols = slice(half * HALF, (half + 1) * HALF)
-                entries = slice(half * HALF // PER_COL, (half + 1) * HALF // PER_COL)
-                nc.scalar.activation(other[:, cols], h[t][:].indirect(n1_l[:, entries]), ACT.Copy)
+            nc.scalar.activation(other[:], h[t][:].indirect(n1_l[:]), ACT.Copy)
             st_t = sb.tile([P, S], F32, name="st%d" % t)
-            nc.vector.tensor_tensor(st_t[:], h[t][:], other[:], ALU.max)
+            nc.vector.tensor_tensor(st_t[:], h[t][:, 0:S], other[:], ALU.max)
             st.append(st_t)
 
-        cand_words, cand_bytes = [], []
+        weighted = sb.tile([P, PACK, S], F32)
+        for t in range(PACK):
+            nc.vector.tensor_scalar(weighted[:, t, :], st[t][:], gain[:, t : t + 1], None, ALU.mult)
 
-        def pick_candidates(t):
-            entries = slice(t * P // PER_COL, (t + 1) * P // PER_COL)
-            words = sb.tile([P, P], U32, align_bytes=64, name="cand_words%d" % t, tag="other2" if t == 0 else "woven1")
-            scale = sb.tile([P, P], U8, align_bytes=64, name="cand_bytes%d" % t, tag="other3" if t == 0 else "planes1")
-            nc.vector.tensor_copy(words[:], x_tab[:].indirect(cand_l[:, entries]))
+        cand_words, cand_bytes = {}, {}
+
+        def pick_words(t, tag):
+            words = sb.tile([P, P], U32, align_bytes=64, name="cand_words%d" % t, tag=tag)
+            nc.vector.tensor_copy(words[:], x_tab[:].indirect(cand_l[:, t * P // PER_COL : (t + 1) * P // PER_COL]))
+            cand_words[t] = words[:]
+
+        def pick_bytes(first, count, tag):
+            scale = sb.tile([P, count * P], U8, align_bytes=64, name="cand_bytes%d" % first, tag=tag)
+            entries = slice(first * P // PER_COL, (first + count) * P // PER_COL)
             nc.vector.tensor_copy(scale[:], x_bytes_cand[:].indirect(cand_l[:, entries]))
-            cand_words.append(words)
-            cand_bytes.append(scale)
+            for i in range(count):
+                cand_bytes[first + i] = scale[:, i * P : (i + 1) * P]
 
-        pick_candidates(0)
+        pick_words(0, "other2")
 
         z_words = sb.tile([P, S], U32, align_bytes=64)
         z_bytes = sb.tile([P, S], U8, align_bytes=64)
         for half in range(2):
             cols = slice(half * HALF, (half + 1) * HALF)
             entries = slice(half * HALF // PER_COL, (half + 1) * HALF // PER_COL)
-            planes = sb.tile([P, PACK, HALF], BF16, align_bytes=64, name="planes%d" % half, tag="planes%d" % half)
+            sg = sb.tile([P, PACK, HALF], F32, align_bytes=64, name="sg%d" % half, tag=("sg0", "other3")[half])
             for t in range(PACK):
-                sg = sb.tile([P, HALF], F32, align_bytes=64, name="sg%d_%d" % (half, t), tag="sg%d_%d" % (half, t))
-                nc.scalar.activation(sg[:], st[t][:].indirect(n2_l[:, entries]), ACT.Sigmoid,
+                nc.scalar.activation(sg[:, t, :], st[t][:].indirect(n2_l[:, entries]), ACT.Sigmoid,
                                      scale=slope[:, t : t + 1], bias=bias[:, t : t + 1])
-                nc.vector.scalar_tensor_tensor(planes[:, t, :], st[t][:, cols], gain[:, t : t + 1], sg[:], ALU.mult, ALU.mult)
-            woven = sb.tile([P, HALF, PACK], BF16, align_bytes=64, name="woven%d" % half, tag="woven%d" % half)
-            nc.vector.tensor_copy(woven[:].rearrange("p (c i) t -> p c t i", i=4), planes[:].rearrange("p t (c i) -> p c t i", i=4))
+            woven = sb.tile([P, HALF, PACK], BF16, align_bytes=64, name="woven%d" % half, tag="woven")
+            nc.vector.tensor_tensor(woven[:].rearrange("p (c i) t -> p c t i", i=4),
+                                    weighted[:, :, cols].rearrange("p t (c i) -> p c t i", i=4),
+                                    sg[:].rearrange("p t (c i) -> p c t i", i=4), ALU.mult)
             nc.vector.quantize_mx(out=z_words[:, cols].bitcast(FP8X4), scales=z_bytes[:, cols],
                                   in_=woven[:].rearrange("p j t -> p (j t)"))
+            if half == 0:
+                pick_bytes(0, 2, "sg0")
 
         s, moved = [], []
 
@@ -155,7 +157,7 @@ def tile_picked_hpqcehhkdif_none_p_kernel(tc, x_words, x_scales, d_words, d_scal
             pieces = [slice(0, HALF), slice(HALF, S)] if t == 0 else [slice(0, S)]
             s_t = sb.tile([P, S], F32, name="s%d" % t)
             for cols in pieces:
-                nc.tensor.matmul_mx(out=acc[:, cols], lhsT=cand_words[t][:].bitcast(FP8X4), lhsT_scale=cand_bytes[t][:],
+                nc.tensor.matmul_mx(out=acc[:, cols], lhsT=cand_words[t].bitcast(FP8X4), lhsT_scale=cand_bytes[t],
                                     rhs=z_words[:, cols].bitcast(FP8X4), rhs_scale=z_bytes[:, cols], start=True, stop=True)
                 if t == 0:
                     nc.scalar.activation(s_t[:, cols], acc[:, cols], ACT.Copy, scale=0.0625)
@@ -164,11 +166,11 @@ def tile_picked_hpqcehhkdif_none_p_kernel(tc, x_words, x_scales, d_words, d_scal
             s.append(s_t)
 
         def fetch(t):
-            old = sb.tile([P, W], F32, name="old%d" % t)
-            partner = sb.tile([P, W], F32, name="partner%d" % t)
+            old = sb.tile([P, W], F32, align_bytes=64, name="old%d" % t, tag="old%d" % t)
+            partner = sb.tile([P, W], F32, align_bytes=64, name="partner%d" % t, tag="partner%d" % t)
             nc.scalar.activation(old[:], s[t][:].indirect(n3_l[:]), ACT.Copy)
             nc.scalar.activation(partner[:], s[t][:].indirect(n4_l[:]), ACT.Copy)
-            new = sb.tile([P, W], F32, align_bytes=64, name="new%d" % t)
+            new = sb.tile([P, W], F32, align_bytes=64, name="new%d" % t, tag=("woven", "old0", "old1", "new3")[t])
             nc.vector.scalar_tensor_tensor(new[:], partner[:], -0.5, old[:], ALU.mult, ALU.add)
             moved.append(new)
 
@@ -179,7 +181,9 @@ def tile_picked_hpqcehhkdif_none_p_kernel(tc, x_words, x_scales, d_words, d_scal
         product(0)
         for t in range(PACK):
             if t + 1 < PACK:
-                pick_candidates(t + 1)
+                pick_words(t + 1, ("woven", "old0", "old1")[t])
+                if t > 0:
+                    pick_bytes(t + 1, 1, "partner%d" % (t - 1))
                 product(t + 1)
             fetch(t)
             if t > 0:

from contextlib import ExitStack

import concourse.mybir as mybir

K, T, S, G, H, C, W = 512, 1024, 256, 2048, 512, 512, 192
FLOPS = 2 * K * H * S + 2 * K * C * S

F32 = mybir.dt.float32
BF16 = mybir.dt.bfloat16
I32 = mybir.dt.int32
U32 = mybir.dt.uint32
U16 = mybir.dt.uint16
U8 = mybir.dt.uint8
FP8X4 = mybir.dt.float8_e4m3fn_x4
ALU = mybir.AluOpType
ACT = mybir.ActivationFunctionType

P = 128
PACK = 4
HALF = S // 2
PER_COL = 16


def tile_picked_hpqcehhkdif_none_p_kernel(tc, x_words, x_scales, d_words, d_scales, sl, th, gs, offs, k1, n1, n2, cand, n3, n4, out):
    nc = tc.nc
    with ExitStack() as ctx:
        lists = ctx.enter_context(tc.tile_pool(name="lists", bufs=1))
        sb = ctx.enter_context(tc.tile_pool(name="sb", bufs=1))
        psum = ctx.enter_context(tc.psum_pool(name="psum", bufs=1))

        def load_list(src, name):
            tile = lists.tile(list(src.shape), U16, name=name)
            nc.sync.dma_start(tile[:], src)
            return tile

        d_bytes = sb.tile([P, G], U8, align_bytes=64)
        x_bytes_runs = sb.tile([P, T], U8, align_bytes=64)
        placed = sb.tile([P, H + S], U8, align_bytes=64)
        nc.vector.memset(x_bytes_runs[:].bitcast(I32), 0)
        nc.vector.memset(d_bytes[:].bitcast(I32), 0)
        x_bytes_cand = sb.tile([P, T], U8, align_bytes=64)
        nc.vector.memset(placed[:].bitcast(I32), 0)
        nc.vector.memset(x_bytes_cand[:].bitcast(I32), 0)

        h = [sb.tile([P, 2 * S], F32, name="h%d" % t) for t in range(PACK)]
        for t in range(PACK):
            nc.vector.memset(h[t][:, S : 2 * S], 0.0)

        d_tab = sb.tile([P, G], U32, align_bytes=64)
        x_tab = sb.tile([P, T], U32, align_bytes=64)
        offs_l = load_list(offs, "offs_l")
        k1_l = load_list(k1, "k1_l")
        nc.sync.dma_start(x_bytes_runs[:].bitcast(I32)[0:P:8, :], x_scales[0].bitcast(I32))
        n1_l = load_list(n1, "n1_l")
        nc.sync.dma_start(d_bytes[:].bitcast(I32)[0:P:8, :], d_scales[0].bitcast(I32))
        nc.sync.dma_start(d_tab[:].bitcast(I32), d_words[0].rearrange("p n t -> p (n t)").bitcast(I32))
        cand_l = load_list(cand, "cand_l")
        nc.sync.dma_start(x_tab[:].bitcast(I32), x_words[0].rearrange("p n t -> p (n t)").bitcast(I32))
        n2_l = load_list(n2, "n2_l")
        n3_l = load_list(n3, "n3_l")
        n4_l = load_list(n4, "n4_l")

        warm_in = sb.tile([P, 1], F32)
        warm_out = sb.tile([P, 1], F32)
        nc.gpsimd.memset(warm_in[:], 0.0)
        nc.scalar.activation(warm_out[:], warm_in[:], ACT.Sigmoid)

        slope = sb.tile([P, PACK], F32)
        thresh = sb.tile([P, PACK], F32)
        gain = sb.tile([P, PACK], F32)
        nc.gpsimd.dma_start(slope[:], sl.rearrange("(p t) o -> p (t o)", t=PACK))
        nc.gpsimd.dma_start(thresh[:], th.rearrange("(p t) o -> p (t o)", t=PACK))
        nc.gpsimd.dma_start(gain[:], gs.rearrange("(p t) o -> p (t o)", t=PACK))
        for q in range(4):
            nc.gpsimd.dma_start(x_bytes_cand[:].bitcast(I32)[32 * q : 32 * q + 4, :], x_scales[0].bitcast(I32)[4 * q : 4 * q + 4, :])
        slope_th = sb.tile([P, PACK], F32)
        bias = sb.tile([P, PACK], F32)
        nc.gpsimd.tensor_tensor(slope_th[:], slope[:], thresh[:], ALU.mult)
        nc.gpsimd.tensor_scalar(bias[:], slope_th[:], -1.0, 0.0, ALU.mult, ALU.add)

        picked_bytes = sb.tile([P, H + S], U8, align_bytes=64)
        nc.vector.tensor_copy(picked_bytes[:, H : H + S], x_bytes_runs[:].indirect(offs_l[:]))
        nc.vector.tensor_copy(picked_bytes[:, 0:H], d_bytes[:].indirect(k1_l[:]))
        for q in range(4):
            (nc.scalar, nc.sync)[q % 2].dma_start(placed[:].bitcast(I32)[32 * q : 32 * q + 4, :], picked_bytes[:].bitcast(I32)[32 * q : 32 * q + 32 : 8, :])

        d_picked = sb.tile([P, H], U32, align_bytes=64)
        x_picked = sb.tile([P, S], U32, align_bytes=64)
        nc.vector.tensor_copy(d_picked[:], d_tab[:].indirect(k1_l[:]))
        nc.vector.tensor_copy(x_picked[:], x_tab[:].indirect(offs_l[:]))

        dealt_words = sb.tile([P, PACK, P], U32, align_bytes=64)
        dealt_bytes = sb.tile([P, PACK, P], U8, align_bytes=64)
        for group in (slice(0, 1), slice(1, 2), slice(2, 4)):
            nc.vector.tensor_copy(dealt_words[:, group, :], d_picked[:].rearrange("p (m t) -> p t m", t=PACK)[:, group, :])
            nc.vector.tensor_copy(dealt_bytes[:, group, :], placed[:, 0:H].rearrange("p (m t) -> p t m", t=PACK)[:, group, :])

        for t in range(PACK):
            acc = psum.tile([P, S], F32, name="h_acc%d" % t)
            nc.tensor.matmul_mx(out=acc[:], lhsT=dealt_words[:, t, :].bitcast(FP8X4), lhsT_scale=dealt_bytes[:, t, :],
                                rhs=x_picked[:].bitcast(FP8X4), rhs_scale=placed[:, H : H + S], start=True, stop=True)
            if t == 0:
                nc.scalar.activation(h[t][:, 0:S], acc[:], ACT.Copy, scale=0.0625)
            else:
                nc.vector.tensor_scalar(h[t][:, 0:S], acc[:], 0.0625, None, ALU.mult)

        st = []
        for t in range(PACK):
            other = sb.tile([P, S], F32, align_bytes=64, name="other%d" % t, tag="other%d" % t)
            nc.scalar.activation(other[:], h[t][:].indirect(n1_l[:]), ACT.Copy)
            st_t = sb.tile([P, S], F32, name="st%d" % t)
            nc.vector.tensor_tensor(st_t[:], h[t][:, 0:S], other[:], ALU.max)
            st.append(st_t)

        weighted = sb.tile([P, PACK, S], F32)
        for t in range(PACK):
            nc.vector.tensor_scalar(weighted[:, t, :], st[t][:], gain[:, t : t + 1], None, ALU.mult)

        cand_words, cand_bytes = {}, {}

        def pick_words(t, tag):
            words = sb.tile([P, P], U32, align_bytes=64, name="cand_words%d" % t, tag=tag)
            nc.vector.tensor_copy(words[:], x_tab[:].indirect(cand_l[:, t * P // PER_COL : (t + 1) * P // PER_COL]))
            cand_words[t] = words[:]

        def pick_bytes(first, count, tag):
            scale = sb.tile([P, count * P], U8, align_bytes=64, name="cand_bytes%d" % first, tag=tag)
            entries = slice(first * P // PER_COL, (first + count) * P // PER_COL)
            nc.vector.tensor_copy(scale[:], x_bytes_cand[:].indirect(cand_l[:, entries]))
            for i in range(count):
                cand_bytes[first + i] = scale[:, i * P : (i + 1) * P]

        pick_words(0, "other2")

        z_words = sb.tile([P, S], U32, align_bytes=64)
        z_bytes = sb.tile([P, S], U8, align_bytes=64)
        for half in range(2):
            cols = slice(half * HALF, (half + 1) * HALF)
            entries = slice(half * HALF // PER_COL, (half + 1) * HALF // PER_COL)
            sg = sb.tile([P, PACK, HALF], F32, align_bytes=64, name="sg%d" % half, tag=("sg0", "other3")[half])
            for t in range(PACK):
                nc.scalar.activation(sg[:, t, :], st[t][:].indirect(n2_l[:, entries]), ACT.Sigmoid,
                                     scale=slope[:, t : t + 1], bias=bias[:, t : t + 1])
            woven = sb.tile([P, HALF, PACK], BF16, align_bytes=64, name="woven%d" % half, tag="woven")
            nc.vector.tensor_tensor(woven[:].rearrange("p (c i) t -> p c t i", i=4),
                                    weighted[:, :, cols].rearrange("p t (c i) -> p c t i", i=4),
                                    sg[:].rearrange("p t (c i) -> p c t i", i=4), ALU.mult)
            nc.vector.quantize_mx(out=z_words[:, cols].bitcast(FP8X4), scales=z_bytes[:, cols],
                                  in_=woven[:].rearrange("p j t -> p (j t)"))
            if half == 0:
                pick_bytes(0, 2, "sg0")

        s, moved = [], []

        def product(t):
            acc = psum.tile([P, S], F32, name="s_acc%d" % t)
            pieces = [slice(0, HALF), slice(HALF, S)] if t == 0 else [slice(0, S)]
            s_t = sb.tile([P, S], F32, name="s%d" % t)
            for cols in pieces:
                nc.tensor.matmul_mx(out=acc[:, cols], lhsT=cand_words[t].bitcast(FP8X4), lhsT_scale=cand_bytes[t],
                                    rhs=z_words[:, cols].bitcast(FP8X4), rhs_scale=z_bytes[:, cols], start=True, stop=True)
                if t == 0:
                    nc.scalar.activation(s_t[:, cols], acc[:, cols], ACT.Copy, scale=0.0625)
                else:
                    nc.vector.tensor_scalar(s_t[:, cols], acc[:, cols], 0.0625, None, ALU.mult)
            s.append(s_t)

        def fetch(t):
            old = sb.tile([P, W], F32, align_bytes=64, name="old%d" % t, tag="old%d" % t)
            partner = sb.tile([P, W], F32, align_bytes=64, name="partner%d" % t, tag="partner%d" % t)
            nc.scalar.activation(old[:], s[t][:].indirect(n3_l[:]), ACT.Copy)
            nc.scalar.activation(partner[:], s[t][:].indirect(n4_l[:]), ACT.Copy)
            new = sb.tile([P, W], F32, align_bytes=64, name="new%d" % t, tag=("woven", "old0", "old1", "new3")[t])
            nc.vector.scalar_tensor_tensor(new[:], partner[:], -0.5, old[:], ALU.mult, ALU.add)
            moved.append(new)

        def put(t):
            nc.scalar.activation(s[t][:].indirect(n3_l[:]), moved[t][:], ACT.Copy)
            nc.sync.dma_start(out[t * P : (t + 1) * P, :], s[t][:])

        product(0)
        for t in range(PACK):
            if t + 1 < PACK:
                pick_words(t + 1, ("woven", "old0", "old1")[t])
                if t > 0:
                    pick_bytes(t + 1, 1, "partner%d" % (t - 1))
                product(t + 1)
            fetch(t)
            if t > 0:
                put(t - 1)
        put(PACK - 1)
